import numpy as np
import ml_dtypes


def mxq(x, axis, fmt="e4m3"):
    dtype, down = {"e4m3": (ml_dtypes.float8_e4m3fn, 7), "e5m2": (ml_dtypes.float8_e5m2, 14)}[fmt]
    v = np.moveaxis(np.asarray(x, np.float32).astype(ml_dtypes.bfloat16).astype(np.float64), axis, -1)
    blocks = v.reshape(v.shape[:-1] + (-1, 32))
    amax = np.abs(blocks).max(-1, keepdims=True)
    byte = np.maximum(np.where(amax > 0, np.frexp(amax)[1] - 1 + 127, 0) - down, 1)
    scale = np.exp2(byte - 127.0)
    codes = (blocks / scale).astype(np.float32).astype(dtype).astype(np.float64)
    return np.moveaxis((codes * scale).reshape(v.shape), -1, axis)


WIDE = False


def mx_kscale(k):
    if not WIDE:
        return np.ones(k)
    levels = np.array([10, -10, 5, -5, 0])
    if k % 512:
        return np.exp2(np.random.permutation(np.resize(levels, k // 32))).repeat(32)
    a = np.empty((k // 512, 16))
    for p in range(k // 512):
        a[p, :8] = np.random.permutation(np.resize(levels, 8))
        for g in range(8):
            far = levels[np.abs(levels - a[p, g]) >= 10]
            a[p, g + 8] = far[np.random.randint(len(far))]
    return np.exp2(a.ravel()).repeat(32)


def f64(x):
    return np.asarray(x).astype(np.float64)


def striped(idx):
    return np.tile(idx.reshape(-1, 16).T, (8, 1)).astype(np.uint16)


def unstriped(offs):
    return offs[:16].T.reshape(-1).astype(np.int64)


def pack_weight(w):
    k, n = w.shape
    w = f64(np.asarray(w, np.float32).astype(ml_dtypes.bfloat16)).reshape(k // 32, 32, n)
    amax = np.abs(w).max(1)
    byte = np.clip(np.where(amax > 0, np.frexp(amax)[1] - 1 + 127 - 7, 1), 1, 254)
    scaled = (w * np.exp2(127.0 - byte)[:, None, :]).reshape(k, n).astype(np.float32)
    words = np.ascontiguousarray(scaled.reshape(k // 512, 128, 4, n).transpose(0, 1, 3, 2)).astype(ml_dtypes.float8_e4m3fn).view(np.uint8)
    return words, np.ascontiguousarray(byte.astype(np.uint8).reshape(k // 512, 16, n))


def unpack_weight(words, scales):
    g, p, n, _ = words.shape
    vals = np.ascontiguousarray(words).view(ml_dtypes.float8_e4m3fn).astype(np.float64) * np.repeat(np.exp2(scales.astype(np.float64) - 127.0), 8, axis=1)[..., None]
    return vals.transpose(0, 1, 3, 2).reshape(g * 512, n)


E2M1 = np.array([0.0, 0.5, 1.0, 1.5, 2.0, 3.0, 4.0, 6.0, -0.0, -0.5, -1.0, -1.5, -2.0, -3.0, -4.0, -6.0])


def pack_fp4(w):
    k, n = w.shape
    w = f64(np.asarray(w, np.float32).astype(ml_dtypes.bfloat16)).reshape(k // 32, 32, n)
    amax = np.abs(w).max(1)
    mant, ex = np.frexp(amax / 6.0)
    byte = np.clip(np.where(amax > 0, np.where(mant > 0.5, ex, ex - 1) + 127, 1), 1, 254)
    scaled = (w * np.exp2(127.0 - byte)[:, None, :]).reshape(k, n).astype(np.float32)
    c = np.ascontiguousarray(scaled.reshape(k // 512, 128, 4, n).transpose(0, 1, 3, 2)).astype(ml_dtypes.float4_e2m1fn).view(np.uint8) & 0xF
    words = (c[..., 0::2] | (c[..., 1::2] << 4)).reshape(k // 512, 128, 2 * n)
    return np.ascontiguousarray(words), np.ascontiguousarray(byte.astype(np.uint8).reshape(k // 512, 16, n))


def unpack_fp4(words, scales):
    g, _, n = scales.shape
    words = np.ascontiguousarray(words).reshape(g, 128, n, 2)
    nib = np.empty((g, 128, n, 4), np.uint8)
    nib[..., 0::2] = words & 0xF
    nib[..., 1::2] = words >> 4
    vals = E2M1[nib] * np.repeat(np.exp2(scales.astype(np.float64) - 127.0), 8, axis=1)[..., None]
    return vals.transpose(0, 1, 3, 2).reshape(g * 512, n)


def planes(y):
    n, m = y.shape
    v = y.astype(np.float32).astype(ml_dtypes.bfloat16).astype(np.float64).reshape(n // 32, 32, m)
    top = np.abs(v).max(1)
    byte = np.clip(np.where(top > 0, np.frexp(top)[1] - 1 + 127 - 7, 1), 1, 254)
    codes = (v * np.exp2(127.0 - byte)[:, None, :]).reshape(n, m).astype(np.float32).astype(ml_dtypes.float8_e4m3fn).view(np.uint8)
    words = codes.reshape(n // 512, 128, 4, m).transpose(0, 1, 3, 2)
    return np.ascontiguousarray(words), np.ascontiguousarray(byte.astype(np.uint8).reshape(n // 512, 16, m))


def sigmoid(v):
    return 1.0 / (1.0 + np.exp(-np.maximum(v, -700.0)))


K, T, S, H, Z, W = 512, 1024, 512, 512, 512, 2048


def setup_inputs():
    n = np.random.standard_normal
    s = mx_kscale(K)[:, None]
    u = mx_kscale(H)
    packed_xT = pack_weight(n((K, T)) * s)
    packed_w1 = pack_fp4(n((K, H)) / np.sqrt(K) / s)
    packed_eT = pack_weight(n((K, W)) * s)
    packed_w2 = pack_fp4(n((K, H)) / np.sqrt(K) / s)
    return {
        "x_words": packed_xT[0],
        "x_scales": packed_xT[1],
        "w1_words": packed_w1[0],
        "w1_scales": packed_w1[1],
        "e_words": packed_eT[0],
        "e_scales": packed_eT[1],
        "w2_words": packed_w2[0],
        "w2_scales": packed_w2[1],
        "unit": (np.random.uniform(0.6, 1.4, (H, 1)) * u[:, None]).astype(np.float32),
        "unit2": (np.random.uniform(0.6, 1.4, (H, 1)) / np.sqrt(H) / u[:, None]).astype(np.float32),
        "offs": striped(np.random.permutation(T)[:S]),
        "rgt": striped(np.random.permutation(W)[:Z]),
        "ln": striped(np.random.permutation(S)),
        "rn": striped(np.random.permutation(Z)),
        "dsp": striped(np.random.permutation(Z)),
    }


def reference(x_words, x_scales, w1_words, w1_scales, e_words, e_scales, w2_words, w2_scales, unit, unit2, offs, rgt, ln, rn, dsp):
    xq = unpack_weight(x_words, x_scales)[:, unstriped(offs)]
    y = unpack_fp4(w1_words, w1_scales).T @ xq
    yl = y[:, unstriped(ln)]
    edl = y - (0.6 * yl)
    hid = f64(unit) * edl
    e_rgt = unpack_weight(e_words, e_scales)[:, unstriped(rgt)]
    ye = unpack_fp4(w2_words, w2_scales).T @ e_rgt
    yr = ye[:, unstriped(rn)]
    edr = ye - (0.6 * yr)
    hid2 = f64(unit2) * edr
    sc = mxq(hid, 0, "e4m3").T @ mxq(hid2, 0, "e4m3")
    sshift = sc[:, unstriped(dsp)]
    gap = sc - sshift
    out_0 = sc * sigmoid(gap)
    return (out_0,) + planes(out_0)

@@ -1,0 +1,285 @@
+from contextlib import ExitStack
+
+import concourse.mybir as mybir
+from concourse.masks import make_identity
+
+F32 = mybir.dt.float32
+BF16 = mybir.dt.bfloat16
+I32 = mybir.dt.int32
+U32 = mybir.dt.uint32
+U16 = mybir.dt.uint16
+U8 = mybir.dt.uint8
+FP8X4 = mybir.dt.float8_e4m3fn_x4
+FP4X4 = mybir.dt.float4_e2m1fn_x4
+ALU = mybir.AluOpType
+ACT = mybir.ActivationFunctionType
+
+P = 128
+PACK = 4
+N = 512
+HALF = N // 2
+T, W = 1024, 2048
+NEIGHBOUR = 0.6
+FLOPS = 3 * 2 * N * N * N
+
+
+def tile_picked_ystrmat_gate_po_kernel(
+    tc, x_words, x_scales, w1_words, w1_scales, e_words, e_scales, w2_words, w2_scales,
+    unit, unit2, offs, rgt, ln, rn, dsp, out_0, out_1, out_2,
+):
+    nc = tc.nc
+    with ExitStack() as ctx:
+        lists = ctx.enter_context(tc.tile_pool(name="lists", bufs=1))
+        sb = ctx.enter_context(tc.tile_pool(name="sb", bufs=1))
+        ps = ctx.enter_context(tc.psum_pool(name="ps", bufs=1))
+
+        def tile(name, cols, dtype):
+            return sb.tile([P, cols], dtype, name=name, align_bytes=64)
+
+        def bank(index, cols):
+            return ps.tile([P, cols], F32, name="bank%d" % index)
+
+        def load_list(name, src):
+            dst = lists.tile([P, N // 16], U16, name=name)
+            nc.sync.dma_start(dst[:], src)
+            return dst
+
+        def zeroed(name, cols, dtype, view):
+            dst = tile(name, cols, dtype)
+            nc.vector.memset(dst[:].bitcast(view), 0)
+            return dst
+
+        def load_scale_rows(queue, dst, src):
+            for q in range(4):
+                queue.dma_start(dst[32 * q : 32 * q + 4, :].bitcast(I32), src[0, 4 * q : 4 * q + 4, :].bitcast(I32))
+
+        xs = zeroed("xs", T, U8, I32)
+        w1s = zeroed("w1s", N, U8, I32)
+        es = zeroed("es", W, U8, I32)
+        w2s = zeroed("w2s", N, U8, I32)
+        unit_rows = tile("unit_rows", P, F32)
+        nc.gpsimd.memset(unit_rows[:], 0.0)
+        ident = tile("ident", P, F32)
+        make_identity(nc, ident[:])
+
+        offs_t = load_list("offs_t", offs)
+        w1w = tile("w1w", 2 * N, U8)
+        nc.sync.dma_start(w1w[:].bitcast(I32), w1_words[0].bitcast(I32))
+        rgt_t = load_list("rgt_t", rgt)
+        load_scale_rows(nc.sync, xs, x_scales)
+        xw = tile("xw", T, I32)
+        nc.sync.dma_start(xw[:], x_words[0].rearrange("p c r -> p (c r)").bitcast(I32))
+        load_scale_rows(nc.sync, w1s, w1_scales)
+        for first, src in ((0, unit), (PACK, unit2)):
+            nc.sync.dma_start(
+                unit_rows[first : first + PACK, :].rearrange("t (g r) -> t g r", r=8),
+                src.rearrange("(g t r) o -> t g (r o)", t=PACK, r=8),
+            )
+        ew = tile("ew", W, I32)
+        nc.sync.dma_start(ew[:], e_words[0].rearrange("p c r -> p (c r)").bitcast(I32))
+        load_scale_rows(nc.sync, es, e_scales)
+        ln_t = load_list("ln_t", ln)
+        w2w = tile("w2w", 2 * N, U8)
+        nc.sync.dma_start(w2w[:].bitcast(I32), w2_words[0].bitcast(I32))
+        load_scale_rows(nc.gpsimd, w2s, w2_scales)
+        rn_t = load_list("rn_t", rn)
+        dsp_t = load_list("dsp_t", dsp)
+
+        unit_ps = bank(7, P)
+        nc.tensor.transpose(unit_ps[:], unit_rows[:], ident[:])
+        unit_cols = tile("unit_cols", 2 * PACK, F32)
+        nc.scalar.copy(unit_cols[:], unit_ps[:, 0 : 2 * PACK])
+
+        def deal(name, raw, cols):
+            dealt = tile(name, cols, U8)
+            nc.vector.tensor_copy(
+                dealt[:].bitcast(I32).rearrange("p (t g r) -> p t g r", t=PACK, g=16),
+                raw[:].bitcast(I32).rearrange("p (g t r) -> p t g r", t=PACK, g=16),
+            )
+            return dealt
+
+        def first_product(side, words, scales, offsets, w_words, w_scales, bank0):
+            picked_s = tile(side + "_picked_s", N, U8)
+            picked_w = tile(side + "_picked_w", N, U32)
+            gathers = [(picked_s[:], scales[:]), (picked_w[:], words[:].bitcast(U32))]
+            for dst, table in gathers if side == "x" else gathers[::-1]:
+                nc.vector.tensor_copy(dst, table.indirect(offsets[:]))
+            dealt_w = deal(side + "_dealt_w", w_words, 2 * N)
+            dealt_s = deal(side + "_dealt_s", w_scales, N)
+            banks = []
+            for t in range(PACK):
+                acc = bank(bank0 + t, N)
+                nc.tensor.matmul_mx(
+                    acc[:],
+                    lhsT=dealt_w[:, 2 * P * t : 2 * P * (t + 1)].bitcast(FP4X4),
+                    lhsT_scale=dealt_s[:, P * t : P * (t + 1)],
+                    rhs=picked_w[:].bitcast(FP8X4),
+                    rhs_scale=picked_s[:],
+                    start=True,
+                    stop=True,
+                )
+                banks.append(acc)
+            return banks
+
+        def half_of(offsets, h):
+            return offsets[:, 16 * h : 16 * (h + 1)]
+
+        def neighbours(side, rows, offsets, h):
+            got = tile("%s_nb%d" % (side, h), PACK * HALF, F32)
+            for t in range(PACK):
+                nc.scalar.activation(
+                    got[:, HALF * t : HALF * (t + 1)],
+                    rows[:, N * t : N * (t + 1)].indirect(half_of(offsets, h)),
+                    ACT.Copy,
+                    scale=-NEIGHBOUR,
+                )
+            return got
+
+        def runs_of_four(ap, width):
+            return ap.rearrange("p (t c i) -> p c t i", t=PACK, i=4)
+
+        y_banks = first_product("x", xw, xs, offs_t, w1w, w1s, 0)
+        y = tile("y", PACK * N, F32)
+        for t in range(PACK):
+            nc.scalar.activation(y[:, N * t : N * (t + 1)], y_banks[t][:], ACT.Copy, scale=unit_cols[:, t : t + 1])
+        y_nb = [neighbours("y", y, ln_t, h) for h in range(2)]
+
+        ye_banks = first_product("e", ew, es, rgt_t, w2w, w2s, PACK)
+        ye = tile("ye", PACK * N, F32)
+        for t in range(PACK):
+            nc.vector.tensor_scalar(
+                ye[:, N * t : N * (t + 1)], ye_banks[t][:], unit_cols[:, PACK + t : PACK + t + 1], None, ALU.mult
+            )
+        ye_nb_all = tile("ye_nb", PACK * N, F32)
+        mid = PACK * HALF
+        nc.vector.tensor_scalar(
+            ye_nb_all[:, mid - HALF : mid + HALF], ye[:].indirect(rn_t[:]), -NEIGHBOUR, 0.0, ALU.mult, ALU.add
+        )
+        for h in range(2):
+            for t in range(1, PACK):
+                first = mid + HALF * t if h == 1 else mid - HALF * (t + 1)
+                nc.scalar.activation(
+                    ye_nb_all[:, first : first + HALF],
+                    ye[:, N * t : N * (t + 1)].indirect(half_of(rn_t, h)),
+                    ACT.Copy,
+                    scale=-NEIGHBOUR,
+                )
+        ye_nb = [
+            runs_of_four(ye_nb_all[:, 0:mid], HALF)[:, :, ::-1, :],
+            runs_of_four(ye_nb_all[:, mid:], HALF),
+        ]
+
+        hid = tile("hid", PACK * N, BF16)
+        for h in range(2):
+            cs = slice(64 * h, 64 * (h + 1))
+            nc.vector.tensor_tensor(
+                hid[:].rearrange("p (i c t) -> p c t i", i=4, t=PACK)[:, cs],
+                runs_of_four(y[:], N)[:, cs],
+                runs_of_four(y_nb[h][:], HALF),
+                ALU.add,
+            )
+        hid_w = tile("hid_w", N, U32)
+        hid_s = tile("hid_s", N, U8)
+        nc.vector.quantize_mx(hid_w[:].bitcast(FP8X4), hid_s[:], hid[:])
+
+        sc = tile("sc", PACK * N, F32)
+        for h in range(2):
+            cs = slice(64 * h, 64 * (h + 1))
+            hid2 = tile("hid2_%d" % h, PACK * HALF, BF16)
+            nc.vector.tensor_tensor(
+                hid2[:].rearrange("p (c i t) -> p c t i", i=4, t=PACK),
+                runs_of_four(ye[:], N)[:, cs],
+                ye_nb[h],
+                ALU.add,
+            )
+            hid2_w = tile("hid2_w%d" % h, HALF, U32)
+            hid2_s = tile("hid2_s%d" % h, HALF, U8)
+            nc.vector.quantize_mx(hid2_w[:].bitcast(FP8X4), hid2_s[:], hid2[:])
+            for r in range(PACK):
+                acc = bank(PACK * h + r, HALF)
+                nc.tensor.matmul_mx(
+                    acc[:],
+                    lhsT=hid_w[:, P * r : P * (r + 1)].bitcast(FP8X4),
+                    lhsT_scale=hid_s[:, P * r : P * (r + 1)],
+                    rhs=hid2_w[:].bitcast(FP8X4),
+                    rhs_scale=hid2_s[:],
+                    start=True,
+                    stop=True,
+                )
+                dst = sc[:, N * r + HALF * h : N * r + HALF * (h + 1)]
+                if h == 1 and r % 2 == 1:
+                    nc.vector.tensor_scalar(dst, acc[:], 0.5, None, ALU.mult)
+                else:
+                    nc.scalar.activation(dst, acc[:], ACT.Copy, scale=0.5)
+
+        out_s = tile("out_s", N, U8)
+        out_rows = out_0.rearrange("(l r) e -> l r e", r=PACK)
+        out_words = out_1[0].rearrange("p c r -> p (c r)").bitcast(I32)
+        sc3 = sc[:].rearrange("p (r e) -> p r e", r=PACK)
+        shift, gap, gate, res = {}, {}, {}, {}
+        for h in range(2):
+            res[h] = tile("res%d" % h, PACK * HALF, F32)
+            for g in range(2):
+                shift[h, g] = tile("shift%d%d" % (h, g), 2 * HALF, F32)
+                gap[h, g] = tile("gap%d%d" % (h, g), 2 * HALF, F32)
+                gate[h, g] = tile("gate%d%d" % (h, g), 2 * HALF, F32)
+
+        def pair(ap):
+            return ap.rearrange("p (r e) -> p r e", r=2)
+
+        def sc_pair(h, g):
+            return sc3[:, 2 * g : 2 * g + 2, HALF * h : HALF * (h + 1)]
+
+        def fetch(h, r):
+            window = sc[:, N * r : N * (r + 1)].indirect(half_of(dsp_t, h))
+            dst = shift[h, r // 2][:, HALF * (r % 2) : HALF * (r % 2 + 1)]
+            if h == 0 and r % 2 == 1:
+                nc.vector.tensor_copy(dst, window)
+            else:
+                nc.scalar.activation(dst, window, ACT.Copy)
+
+        def sub(h, g):
+            nc.vector.tensor_tensor(pair(gap[h, g][:]), sc_pair(h, g), pair(shift[h, g][:]), ALU.subtract)
+
+        def squash(h, g):
+            nc.scalar.activation(gate[h, g][:], gap[h, g][:], ACT.Tanh)
+
+        def mul(h, g):
+            nc.vector.scalar_tensor_tensor(
+                pair(res[h][:, N * g : N * (g + 1)]), pair(gate[h, g][:]), 1.0, sc_pair(h, g), ALU.add, ALU.mult
+            )
+
+        def hand_out(h):
+            cols = slice(HALF * h, HALF * (h + 1))
+            nc.sync.dma_start(out_rows[:, :, cols], res[h][:].rearrange("p (r e) -> p r e", r=PACK))
+            res_bf = tile("res_bf%d" % h, PACK * HALF, BF16)
+            nc.vector.tensor_copy(
+                res_bf[:].rearrange("p (c i t) -> p c t i", i=4, t=PACK), runs_of_four(res[h][:], HALF)
+            )
+            out_w = tile("out_w%d" % h, HALF, U32)
+            nc.vector.quantize_mx(out_w[:].bitcast(FP8X4), out_s[:, cols], res_bf[:])
+            nc.sync.dma_start(out_words[:, cols], out_w[:].bitcast(I32))
+
+        for r in range(PACK):
+            fetch(0, r)
+        sub(0, 0)
+        sub(0, 1)
+        fetch(1, 0)
+        squash(0, 0)
+        fetch(1, 1)
+        squash(0, 1)
+        mul(0, 0)
+        sub(1, 0)
+        mul(0, 1)
+        fetch(1, 2)
+        fetch(1, 3)
+        squash(1, 0)
+        hand_out(0)
+        sub(1, 1)
+        squash(1, 1)
+        mul(1, 0)
+        mul(1, 1)
+        hand_out(1)
+        for q in range(4):
+            queue = nc.sync if q % 2 == 0 else nc.scalar
+            queue.dma_start(out_2[0, 4 * q : 4 * q + 4, :].bitcast(I32), out_s[32 * q : 32 * q + 4, :].bitcast(I32))

@@ -44,23 +44,24 @@ def tile_picked_ystrmat_gate_po_kernel(
             nc.sync.dma_start(dst[:], src)
             return dst
 
-        def zeroed(name, cols, dtype, view):
-            dst = tile(name, cols, dtype)
-            nc.vector.memset(dst[:].bitcast(view), 0)
+        def zeroed(engine, name, cols):
+            dst = tile(name, cols, U8)
+            engine.memset(dst[:].bitcast(I32), 0)
             return dst
 
         def load_scale_rows(queue, dst, src):
             for q in range(4):
                 queue.dma_start(dst[32 * q : 32 * q + 4, :].bitcast(I32), src[0, 4 * q : 4 * q + 4, :].bitcast(I32))
 
-        xs = zeroed("xs", T, U8, I32)
-        w1s = zeroed("w1s", N, U8, I32)
-        es = zeroed("es", W, U8, I32)
-        w2s = zeroed("w2s", N, U8, I32)
+        xs = zeroed(nc.gpsimd, "xs", T)
+        ident = tile("ident", P, F32)
+        nc.gpsimd.memset(ident[:], 0.0)
         unit_rows = tile("unit_rows", P, F32)
         nc.gpsimd.memset(unit_rows[:], 0.0)
-        ident = tile("ident", P, F32)
-        make_identity(nc, ident[:])
+        make_identity(nc, ident[:], nomemset=True)
+        w1s = zeroed(nc.vector, "w1s", N)
+        es = zeroed(nc.vector, "es", W)
+        w2s = zeroed(nc.vector, "w2s", N)
 
         offs_t = load_list("offs_t", offs)
         w1w = tile("w1w", 2 * N, U8)
@@ -69,12 +70,12 @@ def tile_picked_ystrmat_gate_po_kernel(
         load_scale_rows(nc.sync, xs, x_scales)
         xw = tile("xw", T, I32)
         nc.sync.dma_start(xw[:], x_words[0].rearrange("p c r -> p (c r)").bitcast(I32))
-        load_scale_rows(nc.sync, w1s, w1_scales)
         for first, src in ((0, unit), (PACK, unit2)):
             nc.sync.dma_start(
                 unit_rows[first : first + PACK, :].rearrange("t (g r) -> t g r", r=8),
                 src.rearrange("(g t r) o -> t g (r o)", t=PACK, r=8),
             )
+        load_scale_rows(nc.sync, w1s, w1_scales)
         ew = tile("ew", W, I32)
         nc.sync.dma_start(ew[:], e_words[0].rearrange("p c r -> p (c r)").bitcast(I32))
         load_scale_rows(nc.sync, es, e_scales)
@@ -105,7 +106,7 @@ def tile_picked_ystrmat_gate_po_kernel(
             for dst, table in gathers if side == "x" else gathers[::-1]:
                 nc.vector.tensor_copy(dst, table.indirect(offsets[:]))
             dealt_w = deal(side + "_dealt_w", w_words, 2 * N)
-            dealt_s = deal(side + "_dealt_s", w_scales, N)
+            dealt_s = deal("unit_rows" if side == "x" else "e_dealt_s", w_scales, N)
             banks = []
             for t in range(PACK):
                 acc = bank(bank0 + t, N)
@@ -169,7 +170,7 @@ def tile_picked_ystrmat_gate_po_kernel(
             runs_of_four(ye_nb_all[:, mid:], HALF),
         ]
 
-        hid = tile("hid", PACK * N, BF16)
+        hid = tile("e_dealt_w", PACK * N, BF16)
         for h in range(2):
             cs = slice(64 * h, 64 * (h + 1))
             nc.vector.tensor_tensor(
@@ -245,40 +246,47 @@ def tile_picked_ystrmat_gate_po_kernel(
             nc.scalar.activation(gate[h, g][:], gap[h, g][:], ACT.Tanh)
 
         def mul(h, g):
-            nc.vector.scalar_tensor_tensor(
-                pair(res[h][:, N * g : N * (g + 1)]), pair(gate[h, g][:]), 1.0, sc_pair(h, g), ALU.add, ALU.mult
-            )
+            dst = pair(res[h][:, N * g : N * (g + 1)])
+            nc.vector.scalar_tensor_tensor(dst, pair(gate[h, g][:]), 1.0, sc_pair(h, g), ALU.add, ALU.mult)
+            nc.sync.dma_start(out_rows[:, 2 * g : 2 * g + 2, HALF * h : HALF * (h + 1)], dst)
+
+        res_bf = {}
+
+        def round_result(h):
+            res_bf[h] = tile("res_bf%d" % h, PACK * HALF, BF16)
+            dst = res_bf[h][:].rearrange("p (c i t) -> p c t i", i=4, t=PACK)
+            if h == 0:
+                nc.scalar.copy(dst, runs_of_four(res[h][:], HALF))
+            else:
+                nc.vector.tensor_copy(dst, runs_of_four(res[h][:], HALF))
 
         def hand_out(h):
             cols = slice(HALF * h, HALF * (h + 1))
-            nc.sync.dma_start(out_rows[:, :, cols], res[h][:].rearrange("p (r e) -> p r e", r=PACK))
-            res_bf = tile("res_bf%d" % h, PACK * HALF, BF16)
-            nc.vector.tensor_copy(
-                res_bf[:].rearrange("p (c i t) -> p c t i", i=4, t=PACK), runs_of_four(res[h][:], HALF)
-            )
             out_w = tile("out_w%d" % h, HALF, U32)
-            nc.vector.quantize_mx(out_w[:].bitcast(FP8X4), out_s[:, cols], res_bf[:])
+            nc.vector.quantize_mx(out_w[:].bitcast(FP8X4), out_s[:, cols], res_bf[h][:])
             nc.sync.dma_start(out_words[:, cols], out_w[:].bitcast(I32))
 
         for r in range(PACK):
             fetch(0, r)
         sub(0, 0)
-        sub(0, 1)
         fetch(1, 0)
+        sub(0, 1)
         squash(0, 0)
         fetch(1, 1)
-        squash(0, 1)
         mul(0, 0)
+        squash(0, 1)
         sub(1, 0)
-        mul(0, 1)
         fetch(1, 2)
+        mul(0, 1)
         fetch(1, 3)
         squash(1, 0)
-        hand_out(0)
         sub(1, 1)
-        squash(1, 1)
         mul(1, 0)
+        squash(1, 1)
+        round_result(0)
         mul(1, 1)
+        round_result(1)
+        hand_out(0)
         hand_out(1)
         for q in range(4):
             queue = nc.sync if q % 2 == 0 else nc.scalar

@@ -99,86 +99,88 @@ def tile_picked_ystrmat_gate_po_kernel(
             )
             return dealt
 
-        def first_product(side, words, scales, offsets, w_words, w_scales, bank0):
-            picked_s = tile(side + "_picked_s", N, U8)
-            picked_w = tile(side + "_picked_w", N, U32)
-            gathers = [(picked_s[:], scales[:]), (picked_w[:], words[:].bitcast(U32))]
-            for dst, table in gathers if side == "x" else gathers[::-1]:
-                nc.vector.tensor_copy(dst, table.indirect(offsets[:]))
-            dealt_w = deal(side + "_dealt_w", w_words, 2 * N)
-            dealt_s = deal("unit_rows" if side == "x" else "e_dealt_s", w_scales, N)
-            banks = []
-            for t in range(PACK):
-                acc = bank(bank0 + t, N)
-                nc.tensor.matmul_mx(
-                    acc[:],
-                    lhsT=dealt_w[:, 2 * P * t : 2 * P * (t + 1)].bitcast(FP4X4),
-                    lhsT_scale=dealt_s[:, P * t : P * (t + 1)],
-                    rhs=picked_w[:].bitcast(FP8X4),
-                    rhs_scale=picked_s[:],
-                    start=True,
-                    stop=True,
-                )
-                banks.append(acc)
-            return banks
-
         def half_of(offsets, h):
             return offsets[:, 16 * h : 16 * (h + 1)]
 
-        def neighbours(side, rows, offsets, h):
-            got = tile("%s_nb%d" % (side, h), PACK * HALF, F32)
-            for t in range(PACK):
-                nc.scalar.activation(
-                    got[:, HALF * t : HALF * (t + 1)],
-                    rows[:, N * t : N * (t + 1)].indirect(half_of(offsets, h)),
-                    ACT.Copy,
-                    scale=-NEIGHBOUR,
-                )
-            return got
+        def weight_pass(acc, t, dealt_w, dealt_s, words, scales):
+            nc.tensor.matmul_mx(
+                acc[:],
+                lhsT=dealt_w[:, 2 * P * t : 2 * P * (t + 1)].bitcast(FP4X4),
+                lhsT_scale=dealt_s[:, P * t : P * (t + 1)],
+                rhs=words.bitcast(FP8X4),
+                rhs_scale=scales,
+                start=True,
+                stop=True,
+            )
+
+        def fetch_neighbours(dst, rows, t, offsets, h):
+            nc.scalar.activation(
+                dst, rows[:, N * t : N * (t + 1)].indirect(half_of(offsets, h)), ACT.Copy, scale=-NEIGHBOUR
+            )
 
         def runs_of_four(ap, width):
             return ap.rearrange("p (t c i) -> p c t i", t=PACK, i=4)
 
-        y_banks = first_product("x", xw, xs, offs_t, w1w, w1s, 0)
+        x_s = tile("x_s", N, U8)
+        nc.vector.tensor_copy(x_s[:], xs[:].indirect(offs_t[:]))
+        x_w = tile("x_w", N, U32)
+        nc.vector.tensor_copy(x_w[:], xw[:].bitcast(U32).indirect(offs_t[:]))
+        w1_w = deal("w1_w", w1w, 2 * N)
+        w1_s = deal("unit_rows", w1s, N)
         y = tile("y", PACK * N, F32)
         for t in range(PACK):
-            nc.scalar.activation(y[:, N * t : N * (t + 1)], y_banks[t][:], ACT.Copy, scale=unit_cols[:, t : t + 1])
-        y_nb = [neighbours("y", y, ln_t, h) for h in range(2)]
+            acc = bank(t, N)
+            weight_pass(acc, t, w1_w, w1_s, x_w[:], x_s[:])
+            nc.scalar.activation(y[:, N * t : N * (t + 1)], acc[:], ACT.Copy, scale=unit_cols[:, t : t + 1])
+        chunk = PACK * HALF
+        nb = tile("nb", 3 * chunk, F32)
+        for h in range(2):
+            for t in range(PACK):
+                first = chunk * (1 + h) + HALF * t
+                fetch_neighbours(nb[:, first : first + HALF], y, t, ln_t, h)
 
-        ye_banks = first_product("e", ew, es, rgt_t, w2w, w2s, PACK)
+        e_w = tile("e_w", N, U32)
+        nc.vector.tensor_copy(e_w[:], ew[:].bitcast(U32).indirect(rgt_t[:]))
+        w2_w = deal("w2_w", w2w, 2 * N)
+        w2_s = deal("w2_s", w2s, N)
         ye = tile("ye", PACK * N, F32)
-        for t in range(PACK):
-            nc.vector.tensor_scalar(
-                ye[:, N * t : N * (t + 1)], ye_banks[t][:], unit_cols[:, PACK + t : PACK + t + 1], None, ALU.mult
-            )
-        ye_nb_all = tile("ye_nb", PACK * N, F32)
-        mid = PACK * HALF
-        nc.vector.tensor_scalar(
-            ye_nb_all[:, mid - HALF : mid + HALF], ye[:].indirect(rn_t[:]), -NEIGHBOUR, 0.0, ALU.mult, ALU.add
-        )
+        e_s = []
         for h in range(2):
-            for t in range(1, PACK):
-                first = mid + HALF * t if h == 1 else mid - HALF * (t + 1)
-                nc.scalar.activation(
-                    ye_nb_all[:, first : first + HALF],
-                    ye[:, N * t : N * (t + 1)].indirect(half_of(rn_t, h)),
-                    ACT.Copy,
-                    scale=-NEIGHBOUR,
+            e_s.append(tile(("w2s", "w2w")[h], HALF, U8))
+            nc.vector.tensor_copy(e_s[h][:], es[:].indirect(half_of(rgt_t, h)))
+        for h in range(2):
+            for t in range(PACK):
+                acc = bank(PACK * (1 - h) + t, HALF)
+                weight_pass(acc, t, w2_w, w2_s, e_w[:, HALF * h : HALF * (h + 1)], e_s[h][:])
+                first = N * t + HALF * h
+                nc.vector.tensor_scalar(
+                    ye[:, first : first + HALF], acc[:], unit_cols[:, PACK + t : PACK + t + 1], None, ALU.mult
                 )
-        ye_nb = [
-            runs_of_four(ye_nb_all[:, 0:mid], HALF)[:, :, ::-1, :],
-            runs_of_four(ye_nb_all[:, mid:], HALF),
-        ]
 
-        hid = tile("e_dealt_w", PACK * N, BF16)
-        for h in range(2):
+        hid = tile("w2_w", PACK * N, BF16)
+
+        def combine_left(h):
             cs = slice(64 * h, 64 * (h + 1))
             nc.vector.tensor_tensor(
                 hid[:].rearrange("p (i c t) -> p c t i", i=4, t=PACK)[:, cs],
                 runs_of_four(y[:], N)[:, cs],
-                runs_of_four(y_nb[h][:], HALF),
+                runs_of_four(nb[:, chunk * (1 + h) : chunk * (2 + h)], HALF),
                 ALU.add,
             )
+
+        for t in range(1, PACK):
+            fetch_neighbours(nb[:, chunk - HALF * (t + 1) : chunk - HALF * t], ye, t, rn_t, 0)
+        combine_left(0)
+        nc.vector.tensor_scalar(
+            nb[:, chunk - HALF : chunk + HALF], ye[:].indirect(rn_t[:]), -NEIGHBOUR, 0.0, ALU.mult, ALU.add
+        )
+        for t in range(1, PACK):
+            fetch_neighbours(nb[:, chunk + HALF * t : chunk + HALF * (t + 1)], ye, t, rn_t, 1)
+        combine_left(1)
+        ye_nb = [
+            runs_of_four(nb[:, 0:chunk], HALF)[:, :, ::-1, :],
+            runs_of_four(nb[:, chunk : 2 * chunk], HALF),
+        ]
         hid_w = tile("hid_w", N, U32)
         hid_s = tile("hid_s", N, U8)
         nc.vector.quantize_mx(hid_w[:].bitcast(FP8X4), hid_s[:], hid[:])
@@ -281,12 +283,12 @@ def tile_picked_ystrmat_gate_po_kernel(
         fetch(1, 3)
         squash(1, 0)
         sub(1, 1)
+        round_result(0)
         mul(1, 0)
         squash(1, 1)
-        round_result(0)
+        hand_out(0)
         mul(1, 1)
         round_result(1)
-        hand_out(0)
         hand_out(1)
         for q in range(4):
             queue = nc.sync if q % 2 == 0 else nc.scalar

@@ -49,8 +49,8 @@ def tile_picked_ystrmat_gate_po_kernel(
             engine.memset(dst[:].bitcast(I32), 0)
             return dst
 
-        def load_scale_rows(queue, dst, src):
-            for q in range(4):
+        def load_scale_rows(queue, dst, src, quadrants):
+            for q in quadrants:
                 queue.dma_start(dst[32 * q : 32 * q + 4, :].bitcast(I32), src[0, 4 * q : 4 * q + 4, :].bitcast(I32))
 
         xs = zeroed(nc.gpsimd, "xs", T)
@@ -66,8 +66,9 @@ def tile_picked_ystrmat_gate_po_kernel(
         offs_t = load_list("offs_t", offs)
         w1w = tile("w1w", 2 * N, U8)
         nc.sync.dma_start(w1w[:].bitcast(I32), w1_words[0].bitcast(I32))
-        rgt_t = load_list("rgt_t", rgt)
-        load_scale_rows(nc.sync, xs, x_scales)
+        w2w = tile("w2w", 2 * N, U8)
+        nc.sync.dma_start(w2w[:].bitcast(I32), w2_words[0].bitcast(I32))
+        load_scale_rows(nc.sync, xs, x_scales, range(4))
         xw = tile("xw", T, I32)
         nc.sync.dma_start(xw[:], x_words[0].rearrange("p c r -> p (c r)").bitcast(I32))
         for first, src in ((0, unit), (PACK, unit2)):
@@ -75,14 +76,14 @@ def tile_picked_ystrmat_gate_po_kernel(
                 unit_rows[first : first + PACK, :].rearrange("t (g r) -> t g r", r=8),
                 src.rearrange("(g t r) o -> t g (r o)", t=PACK, r=8),
             )
-        load_scale_rows(nc.sync, w1s, w1_scales)
+        load_scale_rows(nc.sync, w1s, w1_scales, range(4))
         ew = tile("ew", W, I32)
         nc.sync.dma_start(ew[:], e_words[0].rearrange("p c r -> p (c r)").bitcast(I32))
-        load_scale_rows(nc.sync, es, e_scales)
+        rgt_t = load_list("rgt_t", rgt)
         ln_t = load_list("ln_t", ln)
-        w2w = tile("w2w", 2 * N, U8)
-        nc.sync.dma_start(w2w[:].bitcast(I32), w2_words[0].bitcast(I32))
-        load_scale_rows(nc.gpsimd, w2s, w2_scales)
+        load_scale_rows(nc.sync, es, e_scales, range(4))
+        load_scale_rows(nc.sync, w2s, w2_scales, range(1))
+        load_scale_rows(nc.gpsimd, w2s, w2_scales, range(1, 4))
         rn_t = load_list("rn_t", rn)
         dsp_t = load_list("dsp_t", dsp)
 
@@ -185,10 +186,11 @@ def tile_picked_ystrmat_gate_po_kernel(
         hid_s = tile("hid_s", N, U8)
         nc.vector.quantize_mx(hid_w[:].bitcast(FP8X4), hid_s[:], hid[:])
 
-        sc = tile("sc", PACK * N, F32)
+        sc = [tile("sc%d" % r, N, F32) for r in range(PACK)]
+        sc_first = tile("sc_first", chunk, F32)
         for h in range(2):
             cs = slice(64 * h, 64 * (h + 1))
-            hid2 = tile("hid2_%d" % h, PACK * HALF, BF16)
+            hid2 = tile("hid2_%d" % h, chunk, BF16)
             nc.vector.tensor_tensor(
                 hid2[:].rearrange("p (c i t) -> p c t i", i=4, t=PACK),
                 runs_of_four(ye[:], N)[:, cs],
@@ -209,87 +211,68 @@ def tile_picked_ystrmat_gate_po_kernel(
                     start=True,
                     stop=True,
                 )
-                dst = sc[:, N * r + HALF * h : N * r + HALF * (h + 1)]
-                if h == 1 and r % 2 == 1:
+                dst = sc[r][:, HALF * h : HALF * (h + 1)]
+                if h == 1 and r < 2:
                     nc.vector.tensor_scalar(dst, acc[:], 0.5, None, ALU.mult)
                 else:
                     nc.scalar.activation(dst, acc[:], ACT.Copy, scale=0.5)
+                if h == 0:
+                    nc.scalar.activation(sc_first[:, HALF * r : HALF * (r + 1)], acc[:], ACT.Copy, scale=0.5)
 
         out_s = tile("out_s", N, U8)
         out_rows = out_0.rearrange("(l r) e -> l r e", r=PACK)
         out_words = out_1[0].rearrange("p c r -> p (c r)").bitcast(I32)
-        sc3 = sc[:].rearrange("p (r e) -> p r e", r=PACK)
-        shift, gap, gate, res = {}, {}, {}, {}
-        for h in range(2):
-            res[h] = tile("res%d" % h, PACK * HALF, F32)
-            for g in range(2):
-                shift[h, g] = tile("shift%d%d" % (h, g), 2 * HALF, F32)
-                gap[h, g] = tile("gap%d%d" % (h, g), 2 * HALF, F32)
-                gate[h, g] = tile("gate%d%d" % (h, g), 2 * HALF, F32)
+        res = [tile("res%d" % h, chunk, F32) for h in range(2)]
+        gap = [tile("gap%d" % h, chunk, F32) for h in range(2)]
+        gate = [tile("gate%d" % h, chunk, F32) for h in range(2)]
+        shift = tile("shift", chunk, F32)
 
-        def pair(ap):
-            return ap.rearrange("p (r e) -> p r e", r=2)
+        def rows(first, count):
+            return slice(HALF * first, HALF * (first + count))
 
-        def sc_pair(h, g):
-            return sc3[:, 2 * g : 2 * g + 2, HALF * h : HALF * (h + 1)]
+        def store_rows(h, first):
+            nc.sync.dma_start(
+                out_rows[:, first : first + 2, HALF * h : HALF * (h + 1)],
+                res[h][:, rows(first, 2)].rearrange("p (r e) -> p r e", r=2),
+            )
 
-        def fetch(h, r):
-            window = sc[:, N * r : N * (r + 1)].indirect(half_of(dsp_t, h))
-            dst = shift[h, r // 2][:, HALF * (r % 2) : HALF * (r % 2 + 1)]
-            if h == 0 and r % 2 == 1:
-                nc.vector.tensor_copy(dst, window)
-            else:
-                nc.scalar.activation(dst, window, ACT.Copy)
+        def round_result(copy, h):
+            rounded = tile("res_bf%d" % h, chunk, BF16)
+            copy(rounded[:].rearrange("p (c i t) -> p c t i", i=4, t=PACK), runs_of_four(res[h][:], HALF))
+            return rounded
 
-        def sub(h, g):
-            nc.vector.tensor_tensor(pair(gap[h, g][:]), sc_pair(h, g), pair(shift[h, g][:]), ALU.subtract)
-
-        def squash(h, g):
-            nc.scalar.activation(gate[h, g][:], gap[h, g][:], ACT.Tanh)
-
-        def mul(h, g):
-            dst = pair(res[h][:, N * g : N * (g + 1)])
-            nc.vector.scalar_tensor_tensor(dst, pair(gate[h, g][:]), 1.0, sc_pair(h, g), ALU.add, ALU.mult)
-            nc.sync.dma_start(out_rows[:, 2 * g : 2 * g + 2, HALF * h : HALF * (h + 1)], dst)
-
-        res_bf = {}
-
-        def round_result(h):
-            res_bf[h] = tile("res_bf%d" % h, PACK * HALF, BF16)
-            dst = res_bf[h][:].rearrange("p (c i t) -> p c t i", i=4, t=PACK)
-            if h == 0:
-                nc.scalar.copy(dst, runs_of_four(res[h][:], HALF))
-            else:
-                nc.vector.tensor_copy(dst, runs_of_four(res[h][:], HALF))
-
-        def hand_out(h):
+        def hand_out(h, rounded):
             cols = slice(HALF * h, HALF * (h + 1))
             out_w = tile("out_w%d" % h, HALF, U32)
-            nc.vector.quantize_mx(out_w[:].bitcast(FP8X4), out_s[:, cols], res_bf[h][:])
+            nc.vector.quantize_mx(out_w[:].bitcast(FP8X4), out_s[:, cols], rounded[:])
             nc.sync.dma_start(out_words[:, cols], out_w[:].bitcast(I32))
 
         for r in range(PACK):
-            fetch(0, r)
-        sub(0, 0)
-        fetch(1, 0)
-        sub(0, 1)
-        squash(0, 0)
-        fetch(1, 1)
-        mul(0, 0)
-        squash(0, 1)
-        sub(1, 0)
-        fetch(1, 2)
-        mul(0, 1)
-        fetch(1, 3)
-        squash(1, 0)
-        sub(1, 1)
-        round_result(0)
-        mul(1, 0)
-        squash(1, 1)
-        hand_out(0)
-        mul(1, 1)
-        round_result(1)
-        hand_out(1)
+            nc.vector.tensor_tensor(
+                gap[0][:, rows(r, 1)], sc[r][:].indirect(half_of(dsp_t, 0)), sc_first[:, rows(r, 1)], ALU.subtract
+            )
+            nc.scalar.activation(shift[:, rows(r, 1)], sc[r][:].indirect(half_of(dsp_t, 1)), ACT.Copy)
+        for r in range(0, PACK, 2):
+            nc.scalar.activation(gate[0][:, rows(r, 2)], gap[0][:, rows(r, 2)], ACT.Tanh, scale=-1.0)
+        for r in range(PACK):
+            nc.vector.tensor_tensor(gap[1][:, rows(r, 1)], sc[r][:, HALF:], shift[:, rows(r, 1)], ALU.subtract)
+        for r in range(0, PACK, 2):
+            nc.vector.scalar_tensor_tensor(
+                res[0][:, rows(r, 2)], gate[0][:, rows(r, 2)], 1.0, sc_first[:, rows(r, 2)], ALU.add, ALU.mult
+            )
+            store_rows(0, r)
+        for r in range(0, PACK, 2):
+            nc.scalar.activation(gate[1][:, rows(r, 2)], gap[1][:, rows(r, 2)], ACT.Tanh)
+        rounded_first = round_result(nc.scalar.copy, 0)
+        for r in range(PACK):
+            nc.vector.scalar_tensor_tensor(
+                res[1][:, rows(r, 1)], gate[1][:, rows(r, 1)], 1.0, sc[r][:, HALF:], ALU.add, ALU.mult
+            )
+            if r % 2 == 1:
+                store_rows(1, r - 1)
+        rounded_second = round_result(nc.vector.tensor_copy, 1)
+        hand_out(0, rounded_first)
+        hand_out(1, rounded_second)
         for q in range(4):
             queue = nc.sync if q % 2 == 0 else nc.scalar
             queue.dma_start(out_2[0, 4 * q : 4 * q + 4, :].bitcast(I32), out_s[32 * q : 32 * q + 4, :].bitcast(I32))

@@ -212,7 +212,7 @@ def tile_picked_ystrmat_gate_po_kernel(
                     stop=True,
                 )
                 dst = sc[r][:, HALF * h : HALF * (h + 1)]
-                if h == 1 and r < 2:
+                if h == 1 and r < 3:
                     nc.vector.tensor_scalar(dst, acc[:], 0.5, None, ALU.mult)
                 else:
                     nc.scalar.activation(dst, acc[:], ACT.Copy, scale=0.5)

from contextlib import ExitStack

import concourse.mybir as mybir
from concourse.masks import make_identity

F32 = mybir.dt.float32
BF16 = mybir.dt.bfloat16
I32 = mybir.dt.int32
U32 = mybir.dt.uint32
U16 = mybir.dt.uint16
U8 = mybir.dt.uint8
FP8X4 = mybir.dt.float8_e4m3fn_x4
FP4X4 = mybir.dt.float4_e2m1fn_x4
ALU = mybir.AluOpType
ACT = mybir.ActivationFunctionType

P = 128
PACK = 4
N = 512
HALF = N // 2
T, W = 1024, 2048
NEIGHBOUR = 0.6
FLOPS = 3 * 2 * N * N * N


def tile_picked_ystrmat_gate_po_kernel(
    tc, x_words, x_scales, w1_words, w1_scales, e_words, e_scales, w2_words, w2_scales,
    unit, unit2, offs, rgt, ln, rn, dsp, out_0, out_1, out_2,
):
    nc = tc.nc
    with ExitStack() as ctx:
        lists = ctx.enter_context(tc.tile_pool(name="lists", bufs=1))
        sb = ctx.enter_context(tc.tile_pool(name="sb", bufs=1))
        ps = ctx.enter_context(tc.psum_pool(name="ps", bufs=1))

        def tile(name, cols, dtype):
            return sb.tile([P, cols], dtype, name=name, align_bytes=64)

        def bank(index, cols):
            return ps.tile([P, cols], F32, name="bank%d" % index)

        def load_list(name, src):
            dst = lists.tile([P, N // 16], U16, name=name)
            nc.sync.dma_start(dst[:], src)
            return dst

        def zeroed(engine, name, cols):
            dst = tile(name, cols, U8)
            engine.memset(dst[:].bitcast(I32), 0)
            return dst

        def load_scale_rows(queue, dst, src, quadrants):
            for q in quadrants:
                queue.dma_start(dst[32 * q : 32 * q + 4, :].bitcast(I32), src[0, 4 * q : 4 * q + 4, :].bitcast(I32))

        xs = zeroed(nc.gpsimd, "xs", T)
        ident = tile("ident", P, F32)
        nc.gpsimd.memset(ident[:], 0.0)
        unit_rows = tile("unit_rows", P, F32)
        nc.gpsimd.memset(unit_rows[:], 0.0)
        make_identity(nc, ident[:], nomemset=True)
        w1s = zeroed(nc.vector, "w1s", N)
        es = zeroed(nc.vector, "es", W)
        w2s = zeroed(nc.vector, "w2s", N)

        offs_t = load_list("offs_t", offs)
        w1w = tile("w1w", 2 * N, U8)
        nc.sync.dma_start(w1w[:].bitcast(I32), w1_words[0].bitcast(I32))
        w2w = tile("w2w", 2 * N, U8)
        nc.sync.dma_start(w2w[:].bitcast(I32), w2_words[0].bitcast(I32))
        load_scale_rows(nc.sync, xs, x_scales, range(4))
        xw = tile("xw", T, I32)
        nc.sync.dma_start(xw[:], x_words[0].rearrange("p c r -> p (c r)").bitcast(I32))
        for first, src in ((0, unit), (PACK, unit2)):
            nc.sync.dma_start(
                unit_rows[first : first + PACK, :].rearrange("t (g r) -> t g r", r=8),
                src.rearrange("(g t r) o -> t g (r o)", t=PACK, r=8),
            )
        load_scale_rows(nc.sync, w1s, w1_scales, range(4))
        ew = tile("ew", W, I32)
        nc.sync.dma_start(ew[:], e_words[0].rearrange("p c r -> p (c r)").bitcast(I32))
        rgt_t = load_list("rgt_t", rgt)
        ln_t = load_list("ln_t", ln)
        load_scale_rows(nc.sync, es, e_scales, range(4))
        load_scale_rows(nc.sync, w2s, w2_scales, range(1))
        load_scale_rows(nc.gpsimd, w2s, w2_scales, range(1, 4))
        rn_t = load_list("rn_t", rn)
        dsp_t = load_list("dsp_t", dsp)

        unit_ps = bank(7, P)
        nc.tensor.transpose(unit_ps[:], unit_rows[:], ident[:])
        unit_cols = tile("unit_cols", 2 * PACK, F32)
        nc.scalar.copy(unit_cols[:], unit_ps[:, 0 : 2 * PACK])

        def deal(name, raw, cols):
            dealt = tile(name, cols, U8)
            nc.vector.tensor_copy(
                dealt[:].bitcast(I32).rearrange("p (t g r) -> p t g r", t=PACK, g=16),
                raw[:].bitcast(I32).rearrange("p (g t r) -> p t g r", t=PACK, g=16),
            )
            return dealt

        def half_of(offsets, h):
            return offsets[:, 16 * h : 16 * (h + 1)]

        def weight_pass(acc, t, dealt_w, dealt_s, words, scales):
            nc.tensor.matmul_mx(
                acc[:],
                lhsT=dealt_w[:, 2 * P * t : 2 * P * (t + 1)].bitcast(FP4X4),
                lhsT_scale=dealt_s[:, P * t : P * (t + 1)],
                rhs=words.bitcast(FP8X4),
                rhs_scale=scales,
                start=True,
                stop=True,
            )

        def fetch_neighbours(dst, rows, t, offsets, h):
            nc.scalar.activation(
                dst, rows[:, N * t : N * (t + 1)].indirect(half_of(offsets, h)), ACT.Copy, scale=-NEIGHBOUR
            )

        def runs_of_four(ap, width):
            return ap.rearrange("p (t c i) -> p c t i", t=PACK, i=4)

        x_s = tile("x_s", N, U8)
        nc.vector.tensor_copy(x_s[:], xs[:].indirect(offs_t[:]))
        x_w = tile("x_w", N, U32)
        nc.vector.tensor_copy(x_w[:], xw[:].bitcast(U32).indirect(offs_t[:]))
        w1_w = deal("w1_w", w1w, 2 * N)
        w1_s = deal("unit_rows", w1s, N)
        y = tile("y", PACK * N, F32)
        for t in range(PACK):
            acc = bank(t, N)
            weight_pass(acc, t, w1_w, w1_s, x_w[:], x_s[:])
            nc.scalar.activation(y[:, N * t : N * (t + 1)], acc[:], ACT.Copy, scale=unit_cols[:, t : t + 1])
        chunk = PACK * HALF
        nb = tile("nb", 3 * chunk, F32)
        for h in range(2):
            for t in range(PACK):
                first = chunk * (1 + h) + HALF * t
                fetch_neighbours(nb[:, first : first + HALF], y, t, ln_t, h)

        e_w = tile("e_w", N, U32)
        nc.vector.tensor_copy(e_w[:], ew[:].bitcast(U32).indirect(rgt_t[:]))
        w2_w = deal("w2_w", w2w, 2 * N)
        w2_s = deal("w2_s", w2s, N)
        ye = tile("ye", PACK * N, F32)
        e_s = []
        for h in range(2):
            e_s.append(tile(("w2s", "w2w")[h], HALF, U8))
            nc.vector.tensor_copy(e_s[h][:], es[:].indirect(half_of(rgt_t, h)))
        for h in range(2):
            for t in range(PACK):
                acc = bank(PACK * (1 - h) + t, HALF)
                weight_pass(acc, t, w2_w, w2_s, e_w[:, HALF * h : HALF * (h + 1)], e_s[h][:])
                first = N * t + HALF * h
                nc.vector.tensor_scalar(
                    ye[:, first : first + HALF], acc[:], unit_cols[:, PACK + t : PACK + t + 1], None, ALU.mult
                )

        hid = tile("w2_w", PACK * N, BF16)

        def combine_left(h):
            cs = slice(64 * h, 64 * (h + 1))
            nc.vector.tensor_tensor(
                hid[:].rearrange("p (i c t) -> p c t i", i=4, t=PACK)[:, cs],
                runs_of_four(y[:], N)[:, cs],
                runs_of_four(nb[:, chunk * (1 + h) : chunk * (2 + h)], HALF),
                ALU.add,
            )

        for t in range(1, PACK):
            fetch_neighbours(nb[:, chunk - HALF * (t + 1) : chunk - HALF * t], ye, t, rn_t, 0)
        combine_left(0)
        nc.vector.tensor_scalar(
            nb[:, chunk - HALF : chunk + HALF], ye[:].indirect(rn_t[:]), -NEIGHBOUR, 0.0, ALU.mult, ALU.add
        )
        for t in range(1, PACK):
            fetch_neighbours(nb[:, chunk + HALF * t : chunk + HALF * (t + 1)], ye, t, rn_t, 1)
        combine_left(1)
        ye_nb = [
            runs_of_four(nb[:, 0:chunk], HALF)[:, :, ::-1, :],
            runs_of_four(nb[:, chunk : 2 * chunk], HALF),
        ]
        hid_w = tile("hid_w", N, U32)
        hid_s = tile("hid_s", N, U8)
        nc.vector.quantize_mx(hid_w[:].bitcast(FP8X4), hid_s[:], hid[:])

        sc = [tile("sc%d" % r, N, F32) for r in range(PACK)]
        sc_first = tile("sc_first", chunk, F32)
        for h in range(2):
            cs = slice(64 * h, 64 * (h + 1))
            hid2 = tile("hid2_%d" % h, chunk, BF16)
            nc.vector.tensor_tensor(
                hid2[:].rearrange("p (c i t) -> p c t i", i=4, t=PACK),
                runs_of_four(ye[:], N)[:, cs],
                ye_nb[h],
                ALU.add,
            )
            hid2_w = tile("hid2_w%d" % h, HALF, U32)
            hid2_s = tile("hid2_s%d" % h, HALF, U8)
            nc.vector.quantize_mx(hid2_w[:].bitcast(FP8X4), hid2_s[:], hid2[:])
            for r in range(PACK):
                acc = bank(PACK * h + r, HALF)
                nc.tensor.matmul_mx(
                    acc[:],
                    lhsT=hid_w[:, P * r : P * (r + 1)].bitcast(FP8X4),
                    lhsT_scale=hid_s[:, P * r : P * (r + 1)],
                    rhs=hid2_w[:].bitcast(FP8X4),
                    rhs_scale=hid2_s[:],
                    start=True,
                    stop=True,
                )
                dst = sc[r][:, HALF * h : HALF * (h + 1)]
                if h == 1 and r < 3:
                    nc.vector.tensor_scalar(dst, acc[:], 0.5, None, ALU.mult)
                else:
                    nc.scalar.activation(dst, acc[:], ACT.Copy, scale=0.5)
                if h == 0:
                    nc.scalar.activation(sc_first[:, HALF * r : HALF * (r + 1)], acc[:], ACT.Copy, scale=0.5)

        out_s = tile("out_s", N, U8)
        out_rows = out_0.rearrange("(l r) e -> l r e", r=PACK)
        out_words = out_1[0].rearrange("p c r -> p (c r)").bitcast(I32)
        res = [tile("res%d" % h, chunk, F32) for h in range(2)]
        gap = [tile("gap%d" % h, chunk, F32) for h in range(2)]
        gate = [tile("gate%d" % h, chunk, F32) for h in range(2)]
        shift = tile("shift", chunk, F32)

        def rows(first, count):
            return slice(HALF * first, HALF * (first + count))

        def store_rows(h, first):
            nc.sync.dma_start(
                out_rows[:, first : first + 2, HALF * h : HALF * (h + 1)],
                res[h][:, rows(first, 2)].rearrange("p (r e) -> p r e", r=2),
            )

        def round_result(copy, h):
            rounded = tile("res_bf%d" % h, chunk, BF16)
            copy(rounded[:].rearrange("p (c i t) -> p c t i", i=4, t=PACK), runs_of_four(res[h][:], HALF))
            return rounded

        def hand_out(h, rounded):
            cols = slice(HALF * h, HALF * (h + 1))
            out_w = tile("out_w%d" % h, HALF, U32)
            nc.vector.quantize_mx(out_w[:].bitcast(FP8X4), out_s[:, cols], rounded[:])
            nc.sync.dma_start(out_words[:, cols], out_w[:].bitcast(I32))

        for r in range(PACK):
            nc.vector.tensor_tensor(
                gap[0][:, rows(r, 1)], sc[r][:].indirect(half_of(dsp_t, 0)), sc_first[:, rows(r, 1)], ALU.subtract
            )
            nc.scalar.activation(shift[:, rows(r, 1)], sc[r][:].indirect(half_of(dsp_t, 1)), ACT.Copy)
        for r in range(0, PACK, 2):
            nc.scalar.activation(gate[0][:, rows(r, 2)], gap[0][:, rows(r, 2)], ACT.Tanh, scale=-1.0)
        for r in range(PACK):
            nc.vector.tensor_tensor(gap[1][:, rows(r, 1)], sc[r][:, HALF:], shift[:, rows(r, 1)], ALU.subtract)
        for r in range(0, PACK, 2):
            nc.vector.scalar_tensor_tensor(
                res[0][:, rows(r, 2)], gate[0][:, rows(r, 2)], 1.0, sc_first[:, rows(r, 2)], ALU.add, ALU.mult
            )
            store_rows(0, r)
        for r in range(0, PACK, 2):
            nc.scalar.activation(gate[1][:, rows(r, 2)], gap[1][:, rows(r, 2)], ACT.Tanh)
        rounded_first = round_result(nc.scalar.copy, 0)
        for r in range(PACK):
            nc.vector.scalar_tensor_tensor(
                res[1][:, rows(r, 1)], gate[1][:, rows(r, 1)], 1.0, sc[r][:, HALF:], ALU.add, ALU.mult
            )
            if r % 2 == 1:
                store_rows(1, r - 1)
        rounded_second = round_result(nc.vector.tensor_copy, 1)
        hand_out(0, rounded_first)
        hand_out(1, rounded_second)
        for q in range(4):
            queue = nc.sync if q % 2 == 0 else nc.scalar
            queue.dma_start(out_2[0, 4 * q : 4 * q + 4, :].bitcast(I32), out_s[32 * q : 32 * q + 4, :].bitcast(I32))
